import numpy as np
import ml_dtypes

BF16 = ml_dtypes.bfloat16


def bf(x):
    return np.asarray(x, np.float32).astype(BF16)


def f32(x):
    return np.asarray(x, np.float32)


def f64(x):
    return np.asarray(x).astype(np.float64)


def striped(idx):
    return np.concatenate([l.reshape(-1, 16).T for l in idx])


def rows(idx, k):
    return np.tile(np.repeat(idx, 16, axis=0), (k // (16 * 8), 1))


def look(tab, idx):
    return np.take_along_axis(f64(tab), rows(idx, len(tab)), axis=1)


K, S, D, V, N, M = 256, 2048, 2, 1024, 2048, 256


def setup_inputs():
    return {"tab": f32(np.random.standard_normal((K, S))), "x0": f32(np.random.standard_normal((K, V))), "w": bf(np.random.standard_normal((K, M)) / np.sqrt(K)), "b": f32(0.5 * np.random.standard_normal((M, 1))), "offs": striped(np.stack([np.random.permutation(S)[:N] for _ in range(8)]))}


def reference(tab, x0, w, b, offs):
    idx = np.stack([g.T.reshape(-1) for g in np.split(offs, 8)])
    x = f64(x0)
    for d in range(D):
        x = np.minimum(x, look(tab, idx[:, d * V:(d + 1) * V]))
    y = f64(w).T @ x
    return np.maximum(y + f64(b), 0.0)

@@ -1,0 +1,90 @@
+import concourse.mybir as mybir
+
+F32 = mybir.dt.float32
+BF16 = mybir.dt.bfloat16
+U16 = mybir.dt.uint16
+
+PARTS = 128
+PIECE = 512
+ENTRIES_PER_COLUMN = 16
+
+FLOPS = 2 * 256 * 256 * 1024
+
+
+def tile_lookup_pool_min_relu_kernel(tc, tab, x0, w, b, offs, out):
+    nc = tc.nc
+    minimum = mybir.AluOpType.min
+    copy = mybir.ActivationFunctionType.Copy
+    relu = mybir.ActivationFunctionType.Relu
+
+    rows, window_columns = tab.shape
+    n_columns = x0.shape[1]
+    n_out = w.shape[1]
+    row_blocks = rows // PARTS
+    out_blocks = n_out // PARTS
+    pieces = n_columns // PIECE
+
+    with (
+        tc.tile_pool(name="held", bufs=1) as held,
+        tc.tile_pool(name="work", bufs=2) as work,
+        tc.psum_pool(name="psum", bufs=1) as psum,
+    ):
+        offsets = held.tile([PARTS, offs.shape[1]], U16, name="offsets")
+        nc.sync.dma_start(offsets[:], offs)
+
+        windows = []
+        centres = []
+        for r in range(row_blocks):
+            block = slice(r * PARTS, (r + 1) * PARTS)
+            window = held.tile([PARTS, window_columns], F32, name=f"window{r}")
+            nc.sync.dma_start(window[:], tab[block, :])
+            centre = held.tile([PARTS, n_columns], F32, name=f"centre{r}")
+            for p in range(pieces):
+                cols = slice(p * PIECE, (p + 1) * PIECE)
+                nc.sync.dma_start(centre[:, cols], x0[block, cols])
+            windows.append(window)
+            centres.append(centre)
+
+        weights = []
+        for r in range(row_blocks):
+            weight = held.tile([PARTS, n_out], BF16, name=f"weight{r}")
+            nc.scalar.dma_start(weight[:], w[r * PARTS : (r + 1) * PARTS, :])
+            weights.append(weight)
+        bias = held.tile([PARTS, out_blocks], F32, name="bias")
+        nc.scalar.dma_start(bias[:], b.rearrange("(m p) o -> p (m o)", p=PARTS))
+
+        sums = {
+            (m, p): psum.tile([PARTS, PIECE], F32, name=f"sum{m}_{p}")
+            for m in range(out_blocks)
+            for p in range(pieces)
+        }
+
+        for r in range(row_blocks):
+            for p in range(pieces):
+                cols = slice(p * PIECE, (p + 1) * PIECE)
+                smallest = centres[r][:, cols]
+                for d in range(2):
+                    first = (d * n_columns + p * PIECE) // ENTRIES_PER_COLUMN
+                    picked = windows[r][:].indirect(
+                        offsets[:, first : first + PIECE // ENTRIES_PER_COLUMN]
+                    )
+                    lower = work.tile([PARTS, PIECE], F32, name=f"lower{d}")
+                    nc.vector.tensor_tensor(lower[:], picked, smallest, minimum)
+                    smallest = lower[:]
+                x = work.tile([PARTS, PIECE], BF16, name="x")
+                nc.scalar.activation(x[:], smallest, copy)
+                for m in range(out_blocks):
+                    nc.tensor.matmul(
+                        sums[m, p][:],
+                        weights[r][:, m * PARTS : (m + 1) * PARTS],
+                        x[:],
+                        start=r == 0,
+                        stop=r == row_blocks - 1,
+                    )
+
+        for p in range(pieces):
+            cols = slice(p * PIECE, (p + 1) * PIECE)
+            for m in range(out_blocks):
+                result = work.tile([PARTS, PIECE], F32, name=f"result{m}")
+                nc.scalar.activation(result[:], sums[m, p][:], relu, bias=bias[:, m : m + 1])
+                nc.sync.dma_start(out[m * PARTS : (m + 1) * PARTS, cols], result[:])

@@ -6,6 +6,7 @@ U16 = mybir.dt.uint16
 
 PARTS = 128
 PIECE = 512
+HALF = PIECE // 2
 ENTRIES_PER_COLUMN = 16
 
 FLOPS = 2 * 256 * 256 * 1024
@@ -14,6 +15,8 @@ FLOPS = 2 * 256 * 256 * 1024
 def tile_lookup_pool_min_relu_kernel(tc, tab, x0, w, b, offs, out):
     nc = tc.nc
     minimum = mybir.AluOpType.min
+    add = mybir.AluOpType.add
+    maximum = mybir.AluOpType.max
     copy = mybir.ActivationFunctionType.Copy
     relu = mybir.ActivationFunctionType.Relu
 
@@ -23,6 +26,7 @@ def tile_lookup_pool_min_relu_kernel(tc, tab, x0, w, b, offs, out):
     row_blocks = rows // PARTS
     out_blocks = n_out // PARTS
     pieces = n_columns // PIECE
+    halves = n_columns // HALF
 
     with (
         tc.tile_pool(name="held", bufs=1) as held,
@@ -34,6 +38,7 @@ def tile_lookup_pool_min_relu_kernel(tc, tab, x0, w, b, offs, out):
 
         windows = []
         centres = []
+        weights = []
         for r in range(row_blocks):
             block = slice(r * PARTS, (r + 1) * PARTS)
             window = held.tile([PARTS, window_columns], F32, name=f"window{r}")
@@ -42,27 +47,25 @@ def tile_lookup_pool_min_relu_kernel(tc, tab, x0, w, b, offs, out):
             for p in range(pieces):
                 cols = slice(p * PIECE, (p + 1) * PIECE)
                 nc.sync.dma_start(centre[:, cols], x0[block, cols])
+            weight = held.tile([PARTS, n_out], BF16, name=f"weight{r}")
+            nc.sync.dma_start(weight[:], w[block, :])
             windows.append(window)
             centres.append(centre)
-
-        weights = []
-        for r in range(row_blocks):
-            weight = held.tile([PARTS, n_out], BF16, name=f"weight{r}")
-            nc.scalar.dma_start(weight[:], w[r * PARTS : (r + 1) * PARTS, :])
             weights.append(weight)
         bias = held.tile([PARTS, out_blocks], F32, name="bias")
-        nc.scalar.dma_start(bias[:], b.rearrange("(m p) o -> p (m o)", p=PARTS))
+        nc.sync.dma_start(bias[:], b.rearrange("(m p) o -> p (m o)", p=PARTS))
 
         sums = {
-            (m, p): psum.tile([PARTS, PIECE], F32, name=f"sum{m}_{p}")
+            (m, h): psum.tile([PARTS, HALF], F32, name=f"sum{m}_{h}")
             for m in range(out_blocks)
-            for p in range(pieces)
+            for h in range(halves)
         }
 
         for r in range(row_blocks):
             for p in range(pieces):
-                cols = slice(p * PIECE, (p + 1) * PIECE)
-                smallest = centres[r][:, cols]
+                vector_is_free = r == row_blocks - 1 and p == pieces - 1
+
+                smallest = centres[r][:, p * PIECE : (p + 1) * PIECE]
                 for d in range(2):
                     first = (d * n_columns + p * PIECE) // ENTRIES_PER_COLUMN
                     picked = windows[r][:].indirect(
@@ -71,20 +74,32 @@ def tile_lookup_pool_min_relu_kernel(tc, tab, x0, w, b, offs, out):
                     lower = work.tile([PARTS, PIECE], F32, name=f"lower{d}")
                     nc.vector.tensor_tensor(lower[:], picked, smallest, minimum)
                     smallest = lower[:]
-                x = work.tile([PARTS, PIECE], BF16, name="x")
-                nc.scalar.activation(x[:], smallest, copy)
-                for m in range(out_blocks):
-                    nc.tensor.matmul(
-                        sums[m, p][:],
-                        weights[r][:, m * PARTS : (m + 1) * PARTS],
-                        x[:],
-                        start=r == 0,
-                        stop=r == row_blocks - 1,
-                    )
 
-        for p in range(pieces):
-            cols = slice(p * PIECE, (p + 1) * PIECE)
-            for m in range(out_blocks):
-                result = work.tile([PARTS, PIECE], F32, name=f"result{m}")
-                nc.scalar.activation(result[:], sums[m, p][:], relu, bias=bias[:, m : m + 1])
-                nc.sync.dma_start(out[m * PARTS : (m + 1) * PARTS, cols], result[:])
+                for h in range(p * PIECE // HALF, (p + 1) * PIECE // HALF):
+                    cols = slice(h * HALF, (h + 1) * HALF)
+                    x = work.tile([PARTS, HALF], BF16, name=f"x{h % 2}")
+                    unrounded = smallest[:, h * HALF - p * PIECE : (h + 1) * HALF - p * PIECE]
+                    if vector_is_free:
+                        nc.vector.tensor_copy(x[:], unrounded)
+                    else:
+                        nc.scalar.activation(x[:], unrounded, copy)
+                    for m in range(out_blocks):
+                        nc.tensor.matmul(
+                            sums[m, h][:],
+                            weights[r][:, m * PARTS : (m + 1) * PARTS],
+                            x[:],
+                            start=r == 0,
+                            stop=r == row_blocks - 1,
+                        )
+
+                    if r == row_blocks - 1:
+                        for m in range(out_blocks):
+                            result = work.tile([PARTS, HALF], F32, name=f"result{m}_{h % 2}")
+                            shift = bias[:, m : m + 1]
+                            if vector_is_free and m % 2 == 1:
+                                nc.vector.tensor_scalar(
+                                    result[:], sums[m, h][:], shift, 0.0, add, maximum
+                                )
+                            else:
+                                nc.scalar.activation(result[:], sums[m, h][:], relu, bias=shift)
+                            nc.sync.dma_start(out[m * PARTS : (m + 1) * PARTS, cols], result[:])

import concourse.mybir as mybir

F32 = mybir.dt.float32
BF16 = mybir.dt.bfloat16
U16 = mybir.dt.uint16

PARTS = 128
PIECE = 512
HALF = PIECE // 2
ENTRIES_PER_COLUMN = 16

FLOPS = 2 * 256 * 256 * 1024


def tile_lookup_pool_min_relu_kernel(tc, tab, x0, w, b, offs, out):
    nc = tc.nc
    minimum = mybir.AluOpType.min
    add = mybir.AluOpType.add
    maximum = mybir.AluOpType.max
    copy = mybir.ActivationFunctionType.Copy
    relu = mybir.ActivationFunctionType.Relu

    rows, window_columns = tab.shape
    n_columns = x0.shape[1]
    n_out = w.shape[1]
    row_blocks = rows // PARTS
    out_blocks = n_out // PARTS
    pieces = n_columns // PIECE
    halves = n_columns // HALF

    with (
        tc.tile_pool(name="held", bufs=1) as held,
        tc.tile_pool(name="work", bufs=2) as work,
        tc.psum_pool(name="psum", bufs=1) as psum,
    ):
        offsets = held.tile([PARTS, offs.shape[1]], U16, name="offsets")
        nc.sync.dma_start(offsets[:], offs)

        windows = []
        centres = []
        weights = []
        for r in range(row_blocks):
            block = slice(r * PARTS, (r + 1) * PARTS)
            window = held.tile([PARTS, window_columns], F32, name=f"window{r}")
            nc.sync.dma_start(window[:], tab[block, :])
            centre = held.tile([PARTS, n_columns], F32, name=f"centre{r}")
            for p in range(pieces):
                cols = slice(p * PIECE, (p + 1) * PIECE)
                nc.sync.dma_start(centre[:, cols], x0[block, cols])
            weight = held.tile([PARTS, n_out], BF16, name=f"weight{r}")
            nc.sync.dma_start(weight[:], w[block, :])
            windows.append(window)
            centres.append(centre)
            weights.append(weight)
        bias = held.tile([PARTS, out_blocks], F32, name="bias")
        nc.sync.dma_start(bias[:], b.rearrange("(m p) o -> p (m o)", p=PARTS))

        sums = {
            (m, h): psum.tile([PARTS, HALF], F32, name=f"sum{m}_{h}")
            for m in range(out_blocks)
            for h in range(halves)
        }

        for r in range(row_blocks):
            for p in range(pieces):
                vector_is_free = r == row_blocks - 1 and p == pieces - 1

                smallest = centres[r][:, p * PIECE : (p + 1) * PIECE]
                for d in range(2):
                    first = (d * n_columns + p * PIECE) // ENTRIES_PER_COLUMN
                    picked = windows[r][:].indirect(
                        offsets[:, first : first + PIECE // ENTRIES_PER_COLUMN]
                    )
                    lower = work.tile([PARTS, PIECE], F32, name=f"lower{d}")
                    nc.vector.tensor_tensor(lower[:], picked, smallest, minimum)
                    smallest = lower[:]

                for h in range(p * PIECE // HALF, (p + 1) * PIECE // HALF):
                    cols = slice(h * HALF, (h + 1) * HALF)
                    x = work.tile([PARTS, HALF], BF16, name=f"x{h % 2}")
                    unrounded = smallest[:, h * HALF - p * PIECE : (h + 1) * HALF - p * PIECE]
                    if vector_is_free:
                        nc.vector.tensor_copy(x[:], unrounded)
                    else:
                        nc.scalar.activation(x[:], unrounded, copy)
                    for m in range(out_blocks):
                        nc.tensor.matmul(
                            sums[m, h][:],
                            weights[r][:, m * PARTS : (m + 1) * PARTS],
                            x[:],
                            start=r == 0,
                            stop=r == row_blocks - 1,
                        )

                    if r == row_blocks - 1:
                        for m in range(out_blocks):
                            result = work.tile([PARTS, HALF], F32, name=f"result{m}_{h % 2}")
                            shift = bias[:, m : m + 1]
                            if vector_is_free and m % 2 == 1:
                                nc.vector.tensor_scalar(
                                    result[:], sums[m, h][:], shift, 0.0, add, maximum
                                )
                            else:
                                nc.scalar.activation(result[:], sums[m, h][:], relu, bias=shift)
                            nc.sync.dma_start(out[m * PARTS : (m + 1) * PARTS, cols], result[:])
